import numpy as np, ml_dtypes
CORES = [78,86,94,102,110,118]
N = 6
import mx_ref
BF = ml_dtypes.bfloat16
def entries(a):
    return np.ascontiguousarray(a.T).reshape(-1)
def table(e):
    return np.ascontiguousarray(np.reshape(e, (-1, 16)).T).astype(np.int32)
def f(rng, *shape):
    return mx_ref.flush((rng.standard_normal(shape, dtype=np.float32) * np.exp2(rng.integers(-2, 3, shape[:-1] + (1,)))).astype(BF))
def wide(rng, *shape, cols=0):
    v = rng.standard_normal(shape, dtype=np.float32) * np.exp2(rng.integers(-12, 13, shape)).astype(np.float32)
    if cols: v *= np.repeat(np.exp2(rng.integers(-cols, cols + 1, shape[:-2] + (1, shape[-1] // 4))) * (rng.random(shape[:-2] + (1, shape[-1] // 4)) > 0.0625), 4, axis=-1).astype(np.float32)
    return mx_ref.flush(v.astype(BF))
SH, CH, RD = 128, 64, 4
def lists(rng, same=False, apart=False, ends=False):
    a = []
    for r in range(N):
        p = rng.permutation(SH); e = []
        for t in range(1, RD):
            if same: c = p[:CH]
            elif apart: c = p[np.arange(CH * (t - 1), CH * t) % SH]
            elif ends: c = np.concatenate([[0, SH - 1], 1 + rng.permutation(SH - 2)[:CH - 2]])
            else: c = rng.permutation(SH)[:CH]
            e.append(rng.permutation(c))
        a.append(table(np.concatenate(e)))
    return {"idx": np.stack(a)}
def setup_inputs(rng):
    return {"wm": f(rng, N, 128, 4 * SH), "dl": f(rng, N, 128, (RD - 1) * 4 * CH), **lists(rng), "x": f(rng, N, 128, RD * 512)}
def setup_inputs_same(rng):
    return {**setup_inputs(rng), **lists(rng, same=True)}
def setup_inputs_apart(rng):
    return {**setup_inputs(rng), **lists(rng, apart=True)}
def setup_inputs_ends(rng):
    return {**setup_inputs(rng), **lists(rng, ends=True)}
def setup_inputs_big(rng):
    d = setup_inputs(rng); d["dl"] = (d["dl"].astype(np.float32) * np.float32(256)).astype(BF); return d
def setup_inputs_spread(rng):
    d = setup_inputs(rng); d["wm"] = wide(rng, N, 128, 4 * SH, cols=8); d["dl"] = wide(rng, N, 128, (RD - 1) * 4 * CH, cols=8); return d
def check_inputs(d):
    b = []
    for r in range(N):
        e = entries(d["idx"][r])
        if e.min() < 0 or e.max() >= SH: b.append("idx: range")
        for t in range(1, RD):
            if len(set(e[CH * (t - 1):CH * t].tolist())) != CH: b.append("idx: a column twice in one round")
    return b
def reference(wm, dl, idx, x):
    W = []
    for q in range(N):
        m = wm[q].reshape(128, SH, 4).copy(); d = dl[q].reshape(128, (RD - 1) * CH, 4); e = entries(idx[q])
        W.append([mx_ref.quantize(wm[q])])
        for t in range(1, RD):
            s = slice(CH * (t - 1), CH * t)
            m[:, e[s]] = (m[:, e[s]].astype(np.float32) + np.float32(0.25) * d[:, s].astype(np.float32)).astype(BF)
            W[q].append(mx_ref.quantize(m.reshape(128, 4 * SH).copy()))
    y = np.zeros((N, 128, RD * N * SH), np.float32)
    for r in range(N):
        for t in range(RD):
            X = mx_ref.quantize(np.ascontiguousarray(x[r][:, 512 * t:512 * t + 512]))
            for q in range(N):
                k = t * N + q
                y[r][:, SH * k:SH * k + SH] = mx_ref.matmul(X, W[q][t])
    return {"y": y}

@@ -1,0 +1,424 @@
+import numpy as np
+from concourse.bass import DstId, RemoteDMATransfer
+from concourse.mybir import dt, AluOpType, ActivationFunctionType
+
+N, SH, CH, RD = 6, 128, 64, 4
+NP = N // 2
+WIN = 2 * SH + 2 * 3 * CH
+F8 = "float8_e4m3fn_x4"
+
+SCRATCH = {
+    "md": ("sbuf", [128, 4 * WIN], "bfloat16"),
+    "dlt": ("sbuf", [128, 3 * 4 * CH], "bfloat16"),
+    "dls": ("sbuf", [128, 3 * 4 * CH], "bfloat16"),
+    "xt": ("sbuf", [128, RD * 512], "bfloat16"),
+    "xq": ("sbuf", [128, RD * 128], F8),
+    "xs": ("sbuf", [128, RD * 128], "uint8"),
+    "wl": ("sbuf", [128, N * SH], F8),
+    "ws": ("sbuf", [128, N * SH], "uint8"),
+    "dq": ("sbuf", [128, N * 3 * CH], F8),
+    "dp": ("sbuf", [128, N * 3 * CH], "uint8"),
+    "hw": ("sbuf", [128, SH], F8),
+    "hws": ("sbuf", [128, SH], "uint8"),
+    "hd": ("sbuf", [128, 3 * CH], F8),
+    "hds": ("sbuf", [128, 3 * CH], "uint8"),
+    "ix": ("sbuf", [128, 12], "int32"),
+    "lo": ("sbuf", [128, 12], "int32"),
+    "hi": ("sbuf", [128, 12], "int32"),
+    "lm": ("sbuf", [128, 12], "int32"),
+    "sm": ("sbuf", [128, 12], "int32"),
+    "piu": ("sbuf", [128, 12], "uint16"),
+    "o1": ("sbuf", [128, 4], "uint16"),
+    "o2": ("sbuf", [128, 4], "uint16"),
+    "o3": ("sbuf", [128, 4], "uint16"),
+    "mi": ("sbuf", [128, CH], "int32"),
+    "mj": ("sbuf", [128, CH], "int32"),
+    "mk": ("sbuf", [128, CH], "float32"),
+    "rm": ("sbuf", [128, CH], "float32"),
+    "vl": ("sbuf", [128, 3 * CH], "float32"),
+    "lw": ("sbuf", [128, 3 * SH], "float32"),
+    "k2": ("sbuf", [128, CH], "float32"),
+    "k3": ("sbuf", [128, CH], "float32"),
+    "c2": ("sbuf", [128, CH], "float32"),
+    "c3": ("sbuf", [128, CH], "float32"),
+    "lu": ("sbuf", [128, 3 * SH], "uint16"),
+    "lsend": ("dram", [128, 3], "uint16"),
+    "lland": ("dram", [N * 128, 3], "uint16"),
+    "comb": ("dram", [16, 3, 8 * N], "uint16"),
+    "offs": ("sbuf", [128, 3 * 8 * N], "uint16"),
+    "pw1": ("sbuf", [128, NP * WIN], "float32"),
+    "pw2": ("sbuf", [128, NP * WIN], "float32"),
+    "pw3": ("sbuf", [128, NP * WIN], "float32"),
+    "y0": ("sbuf", [128, N * SH], "float32"),
+    "y1": ("sbuf", [128, N * SH], "float32"),
+    "y2": ("sbuf", [128, N * SH], "float32"),
+    "y3": ("sbuf", [128, N * SH], "float32"),
+    "pb": ("psum", [128, 512 * 8], "float32"),
+}
+SEMAPHORES = (["vs", "ss", "ps", "gs", "lix", "lwm", "ldl", "lx", "lbo", "st1", "st2", "sty", "stz", "loc", "lst",
+               "hwc", "hwp", "hdc", "hdp"]
+              + ["w%d" % q for q in range(N)] + ["d%d" % q for q in range(N)])
+
+
+def bits(engines):
+    m = 0
+    for e in engines:
+        m |= 1 << e
+    return m
+
+
+def links(src, dst, topo):
+    a, b, d = topo.chip(src), topo.chip(dst), topo.die(src)
+    out = []
+    if not topo.same_plane(a, b):
+        m = [c for c in range(topo.CHIPS) if topo.mates(a, c)][0]
+        out.append(("mate", d, a))
+        a = m
+    if a != b:
+        out.append(("out", d, a))
+        out.append(("in", d, b))
+    return out
+
+
+def helpers(core, dsts, topo):
+    ok = [c for c in topo.cores_of(core) if c != core and all(topo.may_write(c, d) for d in dsts)]
+    near = [c for c in ok if topo.die(c) == topo.die(core)]
+    far = [c for c in ok if topo.die(c) != topo.die(core)]
+    return near[0], far[0]
+
+
+def routes(cores, topo):
+    hp = [helpers(c, [d for d in cores if d != c], topo) for c in cores]
+    far = [[(q + 2) % N, (q + 4) % N] for q in range(N)]
+
+    def cost(sel):
+        load = {}
+        for q in range(N):
+            for r in range(N):
+                if r != q:
+                    s = hp[q][1] if r in sel[q] else cores[q]
+                    for k in links(s, cores[r], topo):
+                        load[k] = load.get(k, 0) + 1
+        return (max(load.values()), sum(v * v for v in load.values()))
+
+    best = cost(far)
+    moved = True
+    while moved:
+        moved = False
+        for q in range(N):
+            for a in range(N):
+                for b in range(a + 1, N):
+                    if q in (a, b):
+                        continue
+                    for q2 in range(N):
+                        for a2 in range(N):
+                            for b2 in range(a2 + 1, N):
+                                if q2 in (a2, b2) or (q2 == q and (a2, b2) != (a, b)) or q2 < q:
+                                    continue
+                                t = [list(f) for f in far]
+                                t[q], t[q2] = [a, b], [a2, b2]
+                                c = cost(t)
+                                if c < best:
+                                    best, far, moved = c, t, True
+    near = [[r for r in range(N) if r != q and r not in far[q]] for q in range(N)]
+    pick = None
+    for n in range(3 ** N):
+        ch = [near[q][n // 3 ** q % 3] for q in range(N)]
+        if pick is None or len(set(ch)) > len(set(pick)):
+            pick = ch
+    return [(hp[q][0], hp[q][1], pick[q], [r for r in near[q] if r != pick[q]], far[q]) for q in range(N)]
+
+
+_CACHE = {}
+
+
+def plan(T, topo):
+    if "r" not in _CACHE:
+        _CACHE["r"] = routes(list(T.cores), topo)
+    return _CACHE["r"]
+
+
+def dst_id(c, topo):
+    rid, pid, _ = topo.addr(c)
+    return DstId(rid=rid, pnc=pid)
+
+
+def u8(v):
+    return v.bitcast(dt.uint8)
+
+
+def helper_program(g, core, T, topo, q, ranks):
+    dst = [T.cores[r] for r in ranks]
+    ids = [dst_id(c, topo) for c in dst]
+    eng = [e for e in topo.engines(core, dst[0]) if all(e in topo.engines(core, d) for d in dst)]
+    wc, dc = slice(SH * q, SH * (q + 1)), slice(3 * CH * q, 3 * CH * (q + 1))
+    n = 0
+    for arr, src, out, sem in ((T.sem.hwc, u8(T.hw[:]), u8(T.wl[:, wc]), "w%d" % q),
+                               (T.sem.hwp, T.hws[:], T.ws[:, wc], "w%d" % q),
+                               (T.sem.hdc, u8(T.hd[:]), u8(T.dq[:, dc]), "d%d" % q),
+                               (T.sem.hdp, T.hds[:], T.dp[:, dc], "d%d" % q)):
+        g.wait_ge(arr, 8)
+        g.remote_dma_fused([RemoteDMATransfer(dst_ids=ids, dma_engine_mask=bits(eng), remote_sem=T.sem[sem],
+                                              srcs=[src], dsts=[out for _ in dst])], local_sem=T.sem.loc)
+        n += len(eng)
+    g.wait_ge(T.sem.loc, n)
+
+
+def rank_program(g, core, T, topo):
+    P = plan(T, topo)
+    r = T.rank_of(core)
+    if r is None:
+        for q in range(N):
+            if core == P[q][0]:
+                helper_program(g, core, T, topo, q, P[q][3])
+            if core == P[q][1]:
+                helper_program(g, core, T, topo, q, P[q][4])
+        return
+    near, far, direct, _, _ = P[r]
+    odd = r % 2
+    mcol = 0 if odd else 512
+    dcol = [None] + [(320 + CH * (k - 1)) if odd else (320 - CH * k) for k in (1, 2, 3)]
+    dlow = 320 if odd else 128
+    gap = (128, 320) if odd else (320, 512)
+    add, mult, ge = AluOpType.add, AluOpType.mult, AluOpType.is_ge
+    cnt = {"v": 0, "s": 0, "p": 0, "g": 0}
+    sem = {"v": T.sem.vs, "s": T.sem.ss, "p": T.sem.ps, "g": T.sem.gs}
+    queue = {"v": g.vector, "s": g.scalar, "p": g.tensor, "g": g, "y": g.sync}
+    seen = {}
+
+    def done(k, ins):
+        ins.then_inc(sem[k], 1)
+        cnt[k] += 1
+        return cnt[k]
+
+    def wait(on, s, val):
+        key = (on, s)
+        if seen.get(key, 0) < val:
+            seen[key] = val
+            queue[on].wait_ge(sem[s] if s in sem else T.sem[s], val)
+
+    v, sc, y, te = g.vector, g.scalar, g.sync, g.tensor
+    wc, dc = slice(SH * r, SH * (r + 1)), slice(3 * CH * r, 3 * CH * (r + 1))
+
+    for k in range(8):
+        sc.dma_start(T.ix[16 * k:16 * k + 16, :], T.idx[:]).then_inc(T.sem.lix, 16)
+    y.dma_start(T.md[:, 4 * mcol:4 * mcol + 512], T.wm[:]).then_inc(T.sem.lwm, 16)
+    y.dma_start(T.dlt[:], T.dl[:]).then_inc(T.sem.ldl, 16)
+    y.dma_start(T.xt[:], T.x[:]).then_inc(T.sem.lx, 16)
+
+    g_mi = done("g", g.iota(T.mi[:], [[-1, CH]], CH, 1))
+    g_lw = done("g", g.iota(T.lw[:], [[1, 16], [0, 3], [16, 8]], mcol, 0, allow_small_or_imprecise_dtypes=True))
+    g_vl = done("g", g.iota(T.vl[:], [[CH if odd else -CH, 3], [1, CH]], dcol[1], 0, allow_small_or_imprecise_dtypes=True))
+    g_rm = done("g", g.iota(T.rm[:], [[0, 4], [1024, 16]], 0, 0, allow_small_or_imprecise_dtypes=True))
+
+    v_gap = done("v", v.memset(T.md[:, 4 * gap[0]:4 * gap[1]], 0.0))
+    wait("v", "g", g_mi)
+    a = done("v", v.tensor_scalar(T.mj[:], T.mi[:], 15, None, AluOpType.bitwise_and))
+    wait("v", "v", a)
+    v_mk = done("v", v.tensor_scalar(T.mk[:], T.mj[:], 0, None, AluOpType.is_equal))
+    wait("v", "lix", 128)
+    v_lo = done("v", v.tensor_scalar(T.lo[:], T.ix[:], 15, None, AluOpType.bitwise_and))
+    v_hi = done("v", v.tensor_scalar(T.hi[:], T.ix[:], 4, None, AluOpType.arith_shift_right))
+    v_o1 = done("v", v.tensor_scalar(T.o1[:], T.ix[:, 0:4], 4, None, mult))
+    wait("v", "v", v_lo)
+    a = done("v", v.tensor_scalar(T.lm[:], T.lo[:], 24, None, mult))
+    wait("v", "v", a)
+    a = done("v", v.tensor_tensor(T.sm[:], T.lm[:], T.hi[:], add))
+    wait("v", "v", a)
+    v_pi = done("v", v.tensor_copy(T.piu[:], T.sm[:]))
+    wait("v", "lwm", 16)
+    v_qw = done("v", v.quantize_mx(T.wl[:, wc], T.ws[:, wc], T.md[:, 4 * mcol:4 * mcol + 512]))
+
+    def place(k, t):
+        wait("v", "v", cnt["v"])
+        return done("v", v.tensor_copy(T.lw[:, 8 * (t - 1):3 * SH].indirect(T.piu[:, 4 * (k - 1):4 * k]),
+                                       T.vl[:, CH * (k - 1):CH * k]))
+
+    def look(t, k, out):
+        wait("v", "v", cnt["v"])
+        return done("v", v.tensor_tensor(out, T.lw[:, 8 * (t - 1):3 * SH].indirect(T.piu[:, 4 * (k - 1):4 * k]),
+                                         T.mk[:], mult))
+
+    wait("v", "g", g_rm)
+    place(1, 1)
+    v_k2 = look(1, 2, T.k2[:])
+    place(1, 2)
+    place(2, 2)
+    v_k3 = look(2, 3, T.k3[:])
+    v_c2 = done("v", v.tensor_tensor_scan(T.c2[:], T.rm[:], T.k2[:], 0.0, AluOpType.min, add))
+    wait("v", "v", v_k3)
+    v_c3 = done("v", v.tensor_tensor_scan(T.c3[:], T.rm[:], T.k3[:], 0.0, AluOpType.min, add))
+    org = [None, mcol, 0 if odd else dcol[1], 0 if odd else dcol[2]]
+    end = [None, mcol + SH, dcol[1] + CH if odd else WIN, dcol[2] + CH if odd else WIN]
+    wait("v", "v", v_c2)
+    done("v", v.tensor_scalar(T.o2[:], T.c2[:, 15:CH:16], -org[2], 4, add, mult))
+    wait("v", "v", v_c3)
+    done("v", v.tensor_scalar(T.o3[:], T.c3[:, 15:CH:16], -org[3], 4, add, mult))
+    for k in (1, 2, 3):
+        wait("v", "v", cnt["v"])
+        wait("v", "s", k)
+        for e in range(4):
+            done("v", v.tensor_tensor(T.md[:, 4 * dcol[k] + e:4 * dcol[k] + 4 * CH:4],
+                                      T.md[:, 4 * org[k] + e:4 * end[k]].indirect(T["o%d" % k][:]),
+                                      T.dls[:, 4 * CH * (k - 1) + e:4 * CH * k:4], add))
+    wait("v", "v", cnt["v"])
+    v_qd = done("v", v.quantize_mx(T.dq[:, dc], T.dp[:, dc], T.md[:, 4 * dlow:4 * dlow + 12 * CH]))
+    place(1, 3)
+    place(2, 3)
+    place(3, 3)
+    wait("v", "v", cnt["v"])
+    v_lu = done("v", v.tensor_copy(T.lu[0:1, :], T.lw[0:1, :]))
+    wait("v", "lx", 16)
+    v_qx = done("v", v.quantize_mx(T.xq[:], T.xs[:], T.xt[:]))
+    for p in range(NP):
+        for t in (1, 2):
+            for lo, hi in ((128, 320 - CH * t), (320 + CH * t, 512)):
+                v_ms = done("v", v.memset(T["pw%d" % t][:, WIN * p + lo:WIN * p + hi], 0.0))
+
+    wait("s", "ldl", 16)
+    for k in range(3):
+        sl = slice(4 * CH * k, 4 * CH * (k + 1))
+        done("s", sc.activation(T.dls[:, sl], T.dlt[:, sl], ActivationFunctionType.Copy, scale=0.25))
+
+    onchip = topo.engines(core, far)
+    ef, en = onchip[0::2], onchip[1::2]
+    drk = T.cores[direct]
+    ed = topo.engines(core, drk)
+    nloc = [0]
+
+    def hand(src, out, s):
+        g.remote_dma_fused([RemoteDMATransfer(dst_ids=[dst_id(far, topo)], dma_engine_mask=bits(ef), remote_sem=T.sem[s],
+                                              srcs=[src], dsts=[out]),
+                            RemoteDMATransfer(dst_ids=[dst_id(near, topo)], dma_engine_mask=bits(en), remote_sem=T.sem[s],
+                                              srcs=[src], dsts=[out])], local_sem=T.sem.loc)
+        nloc[0] += len(ef) + len(en)
+
+    def send(view, s):
+        g.remote_dma_fused([RemoteDMATransfer(dst_ids=[dst_id(drk, topo)], dma_engine_mask=bits(ed), remote_sem=T.sem[s],
+                                              srcs=[view], dsts=[view])], local_sem=T.sem.loc)
+        nloc[0] += len(ed)
+
+    wait("g", "v", v_qw)
+    hand(u8(T.wl[:, wc]), u8(T.hw[:]), "hwc")
+    hand(T.ws[:, wc], T.hws[:], "hwp")
+    send(u8(T.wl[:, wc]), "w%d" % r)
+    send(T.ws[:, wc], "w%d" % r)
+    wait("g", "v", v_qd)
+    hand(u8(T.dq[:, dc]), u8(T.hd[:]), "hdc")
+    hand(T.dp[:, dc], T.hds[:], "hdp")
+    send(u8(T.dq[:, dc]), "d%d" % r)
+    send(T.dp[:, dc], "d%d" % r)
+    others = [T.cores[q] for q in range(N) if q != r]
+    land = T.lland[128 * r:128 * (r + 1), :]
+    wait("g", "lbo", 16)
+    g.remote_dma_fused([RemoteDMATransfer(dst_ids=[dst_id(c, topo) for c in others], dma_engine_mask=bits(ed[:1]),
+                                          remote_sem=T.sem.lst, srcs=[T.lsend[:]], dsts=[land for _ in others])],
+                       local_sem=T.sem.loc)
+    nloc[0] += 1
+
+    wait("y", "v", v_lu)
+    y.dma_start(T.lsend[:], T.lu[0:1, :]).then_inc(T.sem.lbo, 16)
+    wait("y", "lbo", 16)
+    y.dma_start(T.comb[:, :, 8 * r:8 * r + 8], T.lsend[:]).then_inc(T.sem.st1, 16)
+    wait("y", "lst", N - 1)
+    for q in range(N):
+        if q != r:
+            y.dma_start(T.comb[:, :, 8 * q:8 * q + 8], T.lland[128 * q:128 * (q + 1), :]).then_inc(T.sem.st1, 16)
+    wait("y", "st1", 16 * N)
+    for k in range(8):
+        y.dma_start(T.offs[16 * k:16 * k + 16, :], T.comb[:]).then_inc(T.sem.st2, 16)
+
+    order = [(r // 2 + k) % NP for k in range(NP)]
+    units = [("w", p, t) for p in order for t in range(RD)] + [("d", p, t) for p in order for t in (1, 3, 2)]
+    eng = {u: (("s" if u[2] in (0, 2) else "v") if u[0] == "w" else ("v" if u[2] == 3 else "s")) for u in units}
+    bank, use = {}, {"v": 0, "s": 0}
+    for u in units:
+        e = eng[u]
+        bank[u] = (0 if e == "v" else 4) + use[e] % 4
+        use[e] += 1
+    num = {u: i + 1 for i, u in enumerate(units)}
+
+    def ps(u, lo, hi):
+        return T.pb[:, 512 * bank[u] + lo:512 * bank[u] + hi]
+
+    def copy(e, out, in_):
+        return done(e, v.tensor_copy(out, in_) if e == "v" else sc.activation(out, in_, ActivationFunctionType.Copy))
+
+    drained, got, shard = {}, {}, {}
+    pend = []
+
+    def store0():
+        p, k = pend.pop(0)
+        wait("s", "s", k)
+        sc.dma_start(T.y[:, 256 * p:256 * p + 256], T.y0[:, 256 * p:256 * p + 256]).then_inc(T.sem.sty, 16)
+
+    def drain(e, u):
+        kind, p, t = u
+        wait(e, "p", num[u])
+        if kind == "w" and t == 0:
+            drained[u] = copy(e, T.y0[:, 256 * p:256 * p + 256], ps(u, 0, 256))
+        elif kind == "w":
+            copy(e, T["pw%d" % t][:, WIN * p + 512:WIN * p + 640], ps(u, 0, 128))
+            drained[u] = copy(e, T["pw%d" % t][:, WIN * p:WIN * p + 128], ps(u, 128, 256))
+            shard[(p, t)] = (e, drained[u])
+        else:
+            drained[u] = copy(e, T["pw%d" % t][:, WIN * p + 320 - CH * t:WIN * p + 320 + CH * t], ps(u, 0, 128 * t))
+
+    def gather(e, p, t):
+        wait(e, "st2", 128)
+        wait(e, "v", v_ms)
+        wait(e, shard[(p, t)][0], shard[(p, t)][1])
+        wait(e, eng[("d", p, t)], drained[("d", p, t)])
+        win = T["pw%d" % t][:, WIN * p:WIN * p + WIN].indirect(T.offs[:, 48 * (t - 1) + 16 * p:48 * (t - 1) + 16 * p + 16])
+        got[(p, t)] = (e, copy(e, T["y%d" % t][:, 256 * p:256 * p + 256], win))
+
+    for p in order:
+        drain("s", ("w", p, 0))
+        pend.append((p, drained[("w", p, 0)]))
+        drain("s", ("w", p, 2))
+        store0()
+    for p in order:
+        drain("s", ("d", p, 1))
+        drain("s", ("d", p, 2))
+        gather("s", p, 2)
+    for p in order:
+        drain("v", ("w", p, 1))
+        drain("v", ("w", p, 3))
+    for p in order:
+        drain("v", ("d", p, 3))
+        gather("v", p, 1)
+        gather("v", p, 3)
+
+    wait("p", "v", v_qx)
+    last = {}
+    for u in units:
+        kind, p, t = u
+        for q in (2 * p, 2 * p + 1):
+            if q != r:
+                wait("p", ("w%d" if kind == "w" else "d%d") % q, 16)
+        b = bank[u]
+        if b in last:
+            wait("p", eng[u], drained[last[b]])
+        last[b] = u
+        if kind == "w":
+            n, lo = 256, 256 * p
+            codes, scales = T.wl, T.ws
+        else:
+            n, lo = 128 * t, 384 * p + 192 - CH * t
+            codes, scales = T.dq, T.dp
+        done("p", te.matmul_mx(ps(u, 0, n), T.xq[:, 128 * t:128 * t + 128], T.xs[:, 128 * t:128 * t + 128],
+                               codes[:, lo:lo + n], scales[:, lo:lo + n], True, True))
+
+    for p in order:
+        for t in (1, 3, 2):
+            e, k = got[(p, t)]
+            wait("y", e, k)
+            y.dma_start(T.y[:, SH * N * t + 256 * p:SH * N * t + 256 * p + 256],
+                        T["y%d" % t][:, 256 * p:256 * p + 256]).then_inc(T.sem.stz, 16)
+
+    wait("g", "loc", nloc[0])
+    for k in ("g", "v", "s", "p"):
+        wait("g", k, cnt[k])
+    wait("g", "st2", 128)
+    wait("g", "sty", 16 * NP)
+    wait("g", "stz", 16 * 3 * NP)

@@ -28,17 +28,24 @@ SCRATCH = {
     "lm": ("sbuf", [128, 12], "int32"),
     "sm": ("sbuf", [128, 12], "int32"),
     "piu": ("sbuf", [128, 12], "uint16"),
-    "o1": ("sbuf", [128, 4], "uint16"),
-    "o2": ("sbuf", [128, 4], "uint16"),
-    "o3": ("sbuf", [128, 4], "uint16"),
+    "o1": ("sbuf", [128, 16], "uint16"),
+    "o2": ("sbuf", [128, 16], "uint16"),
+    "o3": ("sbuf", [128, 16], "uint16"),
     "mi": ("sbuf", [128, CH], "int32"),
     "mj": ("sbuf", [128, CH], "int32"),
     "mk": ("sbuf", [128, CH], "float32"),
     "rm": ("sbuf", [128, CH], "float32"),
+    "pi": ("sbuf", [128, 1], "int32"),
+    "pe": ("sbuf", [128, 1], "int32"),
+    "e1": ("sbuf", [128, 1], "float32"),
+    "e2": ("sbuf", [128, 1], "float32"),
+    "e3": ("sbuf", [128, 1], "float32"),
     "vl": ("sbuf", [128, 3 * CH], "float32"),
     "lw": ("sbuf", [128, 3 * SH], "float32"),
+    "k1": ("sbuf", [128, CH], "float32"),
     "k2": ("sbuf", [128, CH], "float32"),
     "k3": ("sbuf", [128, CH], "float32"),
+    "c1": ("sbuf", [128, CH], "float32"),
     "c2": ("sbuf", [128, CH], "float32"),
     "c3": ("sbuf", [128, CH], "float32"),
     "lu": ("sbuf", [128, 3 * SH], "uint16"),
@@ -180,7 +187,9 @@ def rank_program(g, core, T, topo):
     dcol = [None] + [(320 + CH * (k - 1)) if odd else (320 - CH * k) for k in (1, 2, 3)]
     dlow = 320 if odd else 128
     gap = (128, 320) if odd else (320, 512)
-    add, mult, ge = AluOpType.add, AluOpType.mult, AluOpType.is_ge
+    org = [None, mcol, 0 if odd else dcol[1], 0 if odd else dcol[2]]
+    end = [None, mcol + SH, dcol[1] + CH if odd else WIN, dcol[2] + CH if odd else WIN]
+    add, mult = AluOpType.add, AluOpType.mult
     cnt = {"v": 0, "s": 0, "p": 0, "g": 0}
     sem = {"v": T.sem.vs, "s": T.sem.ss, "p": T.sem.ps, "g": T.sem.gs}
     queue = {"v": g.vector, "s": g.scalar, "p": g.tensor, "g": g, "y": g.sync}
@@ -200,74 +209,76 @@ def rank_program(g, core, T, topo):
     v, sc, y, te = g.vector, g.scalar, g.sync, g.tensor
     wc, dc = slice(SH * r, SH * (r + 1)), slice(3 * CH * r, 3 * CH * (r + 1))
 
-    for k in range(8):
-        sc.dma_start(T.ix[16 * k:16 * k + 16, :], T.idx[:]).then_inc(T.sem.lix, 16)
+    for k in range(4):
+        y.dma_start(T.ix[16 * k:16 * k + 16, :], T.idx[:]).then_inc(T.sem.lix, 16)
+        sc.dma_start(T.ix[64 + 16 * k:64 + 16 * k + 16, :], T.idx[:]).then_inc(T.sem.lix, 16)
     y.dma_start(T.md[:, 4 * mcol:4 * mcol + 512], T.wm[:]).then_inc(T.sem.lwm, 16)
-    y.dma_start(T.dlt[:], T.dl[:]).then_inc(T.sem.ldl, 16)
+    sc.dma_start(T.dlt[:], T.dl[:]).then_inc(T.sem.ldl, 16)
     y.dma_start(T.xt[:], T.x[:]).then_inc(T.sem.lx, 16)
 
-    g_mi = done("g", g.iota(T.mi[:], [[-1, CH]], CH, 1))
+    g_pi = done("g", g.iota(T.pi[:], [[0, 1]], 0, 1))
+    g_mi = done("g", g.iota(T.mi[:], [[-4, CH]], 4 * CH, 1))
     g_lw = done("g", g.iota(T.lw[:], [[1, 16], [0, 3], [16, 8]], mcol, 0, allow_small_or_imprecise_dtypes=True))
     g_vl = done("g", g.iota(T.vl[:], [[CH if odd else -CH, 3], [1, CH]], dcol[1], 0, allow_small_or_imprecise_dtypes=True))
-    g_rm = done("g", g.iota(T.rm[:], [[0, 4], [1024, 16]], 0, 0, allow_small_or_imprecise_dtypes=True))
+    g_rm = done("g", g.iota(T.rm[:], [[0, 16], [1024, 4]], 0, 0, allow_small_or_imprecise_dtypes=True))
 
-    v_gap = done("v", v.memset(T.md[:, 4 * gap[0]:4 * gap[1]], 0.0))
+    done("v", v.memset(T.md[:, 4 * gap[0]:4 * gap[1]], 0.0))
     wait("v", "g", g_mi)
-    a = done("v", v.tensor_scalar(T.mj[:], T.mi[:], 15, None, AluOpType.bitwise_and))
-    wait("v", "v", a)
-    v_mk = done("v", v.tensor_scalar(T.mk[:], T.mj[:], 0, None, AluOpType.is_equal))
+    v_pe = done("v", v.tensor_scalar(T.pe[:], T.pi[:], 3, None, AluOpType.bitwise_and))
+    v_mj = done("v", v.tensor_scalar(T.mj[:], T.mi[:], 2, 3, AluOpType.arith_shift_right, AluOpType.bitwise_and))
+    wait("v", "v", v_pe)
+    for k in (1, 2, 3):
+        done("v", v.tensor_scalar(T["e%d" % k][:], T.pe[:], -4 * org[k], None, add))
+    wait("v", "v", v_mj)
+    done("v", v.tensor_scalar(T.mk[:], T.mj[:], 0, None, AluOpType.is_equal))
     wait("v", "lix", 128)
     v_lo = done("v", v.tensor_scalar(T.lo[:], T.ix[:], 15, None, AluOpType.bitwise_and))
-    v_hi = done("v", v.tensor_scalar(T.hi[:], T.ix[:], 4, None, AluOpType.arith_shift_right))
-    v_o1 = done("v", v.tensor_scalar(T.o1[:], T.ix[:, 0:4], 4, None, mult))
+    done("v", v.tensor_scalar(T.hi[:], T.ix[:], 4, None, AluOpType.arith_shift_right))
     wait("v", "v", v_lo)
     a = done("v", v.tensor_scalar(T.lm[:], T.lo[:], 24, None, mult))
     wait("v", "v", a)
     a = done("v", v.tensor_tensor(T.sm[:], T.lm[:], T.hi[:], add))
     wait("v", "v", a)
-    v_pi = done("v", v.tensor_copy(T.piu[:], T.sm[:]))
-    wait("v", "lwm", 16)
-    v_qw = done("v", v.quantize_mx(T.wl[:, wc], T.ws[:, wc], T.md[:, 4 * mcol:4 * mcol + 512]))
+    done("v", v.tensor_copy(T.piu[:], T.sm[:]))
 
     def place(k, t):
         wait("v", "v", cnt["v"])
         return done("v", v.tensor_copy(T.lw[:, 8 * (t - 1):3 * SH].indirect(T.piu[:, 4 * (k - 1):4 * k]),
                                        T.vl[:, CH * (k - 1):CH * k]))
 
-    def look(t, k, out):
+    def look(t, k):
         wait("v", "v", cnt["v"])
-        return done("v", v.tensor_tensor(out, T.lw[:, 8 * (t - 1):3 * SH].indirect(T.piu[:, 4 * (k - 1):4 * k]),
+        return done("v", v.tensor_tensor(T["k%d" % k][:], T.lw[:, 8 * (t - 1):3 * SH].indirect(T.piu[:, 4 * (k - 1):4 * k]),
                                          T.mk[:], mult))
 
     wait("v", "g", g_rm)
+    look(3, 1)
     place(1, 1)
-    v_k2 = look(1, 2, T.k2[:])
+    look(1, 2)
+    wait("v", "lwm", 16)
+    v_qw = done("v", v.quantize_mx(T.wl[:, wc], T.ws[:, wc], T.md[:, 4 * mcol:4 * mcol + 512]))
     place(1, 2)
     place(2, 2)
-    v_k3 = look(2, 3, T.k3[:])
-    v_c2 = done("v", v.tensor_tensor_scan(T.c2[:], T.rm[:], T.k2[:], 0.0, AluOpType.min, add))
-    wait("v", "v", v_k3)
-    v_c3 = done("v", v.tensor_tensor_scan(T.c3[:], T.rm[:], T.k3[:], 0.0, AluOpType.min, add))
-    org = [None, mcol, 0 if odd else dcol[1], 0 if odd else dcol[2]]
-    end = [None, mcol + SH, dcol[1] + CH if odd else WIN, dcol[2] + CH if odd else WIN]
-    wait("v", "v", v_c2)
-    done("v", v.tensor_scalar(T.o2[:], T.c2[:, 15:CH:16], -org[2], 4, add, mult))
-    wait("v", "v", v_c3)
-    done("v", v.tensor_scalar(T.o3[:], T.c3[:, 15:CH:16], -org[3], 4, add, mult))
-    for k in (1, 2, 3):
-        wait("v", "v", cnt["v"])
-        wait("v", "s", k)
-        for e in range(4):
-            done("v", v.tensor_tensor(T.md[:, 4 * dcol[k] + e:4 * dcol[k] + 4 * CH:4],
-                                      T.md[:, 4 * org[k] + e:4 * end[k]].indirect(T["o%d" % k][:]),
-                                      T.dls[:, 4 * CH * (k - 1) + e:4 * CH * k:4], add))
-    wait("v", "v", cnt["v"])
-    v_qd = done("v", v.quantize_mx(T.dq[:, dc], T.dp[:, dc], T.md[:, 4 * dlow:4 * dlow + 12 * CH]))
+    look(2, 3)
     place(1, 3)
     place(2, 3)
     place(3, 3)
     wait("v", "v", cnt["v"])
     v_lu = done("v", v.tensor_copy(T.lu[0:1, :], T.lw[0:1, :]))
+    scan = {}
+    for k in (1, 2, 3):
+        scan[k] = done("v", v.tensor_tensor_scan(T["c%d" % k][:], T.rm[:], T["k%d" % k][:], 0.0, AluOpType.min, add))
+    for k in (1, 2, 3):
+        wait("v", "v", scan[k])
+        done("v", v.tensor_scalar(T["o%d" % k][:], T["c%d" % k][:, 3:CH:4], 4, T["e%d" % k][:], mult, add))
+    for k in (1, 2, 3):
+        wait("v", "v", cnt["v"])
+        wait("v", "s", k)
+        done("v", v.tensor_tensor(T.md[:, 4 * dcol[k]:4 * dcol[k] + 4 * CH],
+                                  T.md[:, 4 * org[k]:4 * end[k]].indirect(T["o%d" % k][:]),
+                                  T.dls[:, 4 * CH * (k - 1):4 * CH * k], add))
+    wait("v", "v", cnt["v"])
+    v_qd = done("v", v.quantize_mx(T.dq[:, dc], T.dp[:, dc], T.md[:, 4 * dlow:4 * dlow + 12 * CH]))
     wait("v", "lx", 16)
     v_qx = done("v", v.quantize_mx(T.xq[:], T.xs[:], T.xt[:]))
     for p in range(NP):
@@ -303,11 +314,6 @@ def rank_program(g, core, T, topo):
     hand(T.ws[:, wc], T.hws[:], "hwp")
     send(u8(T.wl[:, wc]), "w%d" % r)
     send(T.ws[:, wc], "w%d" % r)
-    wait("g", "v", v_qd)
-    hand(u8(T.dq[:, dc]), u8(T.hd[:]), "hdc")
-    hand(T.dp[:, dc], T.hds[:], "hdp")
-    send(u8(T.dq[:, dc]), "d%d" % r)
-    send(T.dp[:, dc], "d%d" % r)
     others = [T.cores[q] for q in range(N) if q != r]
     land = T.lland[128 * r:128 * (r + 1), :]
     wait("g", "lbo", 16)
@@ -315,6 +321,11 @@ def rank_program(g, core, T, topo):
                                           remote_sem=T.sem.lst, srcs=[T.lsend[:]], dsts=[land for _ in others])],
                        local_sem=T.sem.loc)
     nloc[0] += 1
+    wait("g", "v", v_qd)
+    hand(u8(T.dq[:, dc]), u8(T.hd[:]), "hdc")
+    hand(T.dp[:, dc], T.hds[:], "hdp")
+    send(u8(T.dq[:, dc]), "d%d" % r)
+    send(T.dp[:, dc], "d%d" % r)
 
     wait("y", "v", v_lu)
     y.dma_start(T.lsend[:], T.lu[0:1, :]).then_inc(T.sem.lbo, 16)
@@ -345,12 +356,6 @@ def rank_program(g, core, T, topo):
         return done(e, v.tensor_copy(out, in_) if e == "v" else sc.activation(out, in_, ActivationFunctionType.Copy))
 
     drained, got, shard = {}, {}, {}
-    pend = []
-
-    def store0():
-        p, k = pend.pop(0)
-        wait("s", "s", k)
-        sc.dma_start(T.y[:, 256 * p:256 * p + 256], T.y0[:, 256 * p:256 * p + 256]).then_inc(T.sem.sty, 16)
 
     def drain(e, u):
         kind, p, t = u
@@ -374,20 +379,28 @@ def rank_program(g, core, T, topo):
 
     for p in order:
         drain("s", ("w", p, 0))
-        pend.append((p, drained[("w", p, 0)]))
         drain("s", ("w", p, 2))
-        store0()
-    for p in order:
-        drain("s", ("d", p, 1))
-        drain("s", ("d", p, 2))
-        gather("s", p, 2)
-    for p in order:
+        wait("s", "s", drained[("w", p, 0)])
+        sc.dma_start(T.y[:, 256 * p:256 * p + 256], T.y0[:, 256 * p:256 * p + 256]).then_inc(T.sem.sty, 16)
         drain("v", ("w", p, 1))
         drain("v", ("w", p, 3))
-    for p in order:
+    A, B, C = order
+    for p in (A, B):
+        drain("s", ("d", p, 1))
+        drain("s", ("d", p, 2))
         drain("v", ("d", p, 3))
-        gather("v", p, 1)
-        gather("v", p, 3)
+    gather("v", A, 1)
+    gather("v", A, 3)
+    gather("s", A, 2)
+    gather("v", B, 3)
+    gather("s", B, 1)
+    gather("s", B, 2)
+    drain("s", ("d", C, 1))
+    drain("s", ("d", C, 2))
+    drain("v", ("d", C, 3))
+    gather("s", C, 2)
+    gather("v", C, 1)
+    gather("v", C, 3)
 
     wait("p", "v", v_qx)
     last = {}
@@ -409,12 +422,11 @@ def rank_program(g, core, T, topo):
         done("p", te.matmul_mx(ps(u, 0, n), T.xq[:, 128 * t:128 * t + 128], T.xs[:, 128 * t:128 * t + 128],
                                codes[:, lo:lo + n], scales[:, lo:lo + n], True, True))
 
-    for p in order:
-        for t in (1, 3, 2):
-            e, k = got[(p, t)]
-            wait("y", e, k)
-            y.dma_start(T.y[:, SH * N * t + 256 * p:SH * N * t + 256 * p + 256],
-                        T["y%d" % t][:, 256 * p:256 * p + 256]).then_inc(T.sem.stz, 16)
+    for p, t in ((A, 1), (A, 2), (A, 3), (B, 1), (B, 3), (B, 2), (C, 1), (C, 2), (C, 3)):
+        e, k = got[(p, t)]
+        wait("y", e, k)
+        y.dma_start(T.y[:, SH * N * t + 256 * p:SH * N * t + 256 * p + 256],
+                    T["y%d" % t][:, 256 * p:256 * p + 256]).then_inc(T.sem.stz, 16)
 
     wait("g", "loc", nloc[0])
     for k in ("g", "v", "s", "p"):

import numpy as np
from concourse.bass import DstId, RemoteDMATransfer
from concourse.mybir import dt, AluOpType, ActivationFunctionType

N, SH, CH, RD = 6, 128, 64, 4
NP = N // 2
WIN = 2 * SH + 2 * 3 * CH
F8 = "float8_e4m3fn_x4"

SCRATCH = {
    "md": ("sbuf", [128, 4 * WIN], "bfloat16"),
    "dlt": ("sbuf", [128, 3 * 4 * CH], "bfloat16"),
    "dls": ("sbuf", [128, 3 * 4 * CH], "bfloat16"),
    "xt": ("sbuf", [128, RD * 512], "bfloat16"),
    "xq": ("sbuf", [128, RD * 128], F8),
    "xs": ("sbuf", [128, RD * 128], "uint8"),
    "wl": ("sbuf", [128, N * SH], F8),
    "ws": ("sbuf", [128, N * SH], "uint8"),
    "dq": ("sbuf", [128, N * 3 * CH], F8),
    "dp": ("sbuf", [128, N * 3 * CH], "uint8"),
    "hw": ("sbuf", [128, SH], F8),
    "hws": ("sbuf", [128, SH], "uint8"),
    "hd": ("sbuf", [128, 3 * CH], F8),
    "hds": ("sbuf", [128, 3 * CH], "uint8"),
    "ix": ("sbuf", [128, 12], "int32"),
    "lo": ("sbuf", [128, 12], "int32"),
    "hi": ("sbuf", [128, 12], "int32"),
    "lm": ("sbuf", [128, 12], "int32"),
    "sm": ("sbuf", [128, 12], "int32"),
    "piu": ("sbuf", [128, 12], "uint16"),
    "o1": ("sbuf", [128, 16], "uint16"),
    "o2": ("sbuf", [128, 16], "uint16"),
    "o3": ("sbuf", [128, 16], "uint16"),
    "mi": ("sbuf", [128, CH], "int32"),
    "mj": ("sbuf", [128, CH], "int32"),
    "mk": ("sbuf", [128, CH], "float32"),
    "rm": ("sbuf", [128, CH], "float32"),
    "pi": ("sbuf", [128, 1], "int32"),
    "pe": ("sbuf", [128, 1], "int32"),
    "e1": ("sbuf", [128, 1], "float32"),
    "e2": ("sbuf", [128, 1], "float32"),
    "e3": ("sbuf", [128, 1], "float32"),
    "vl": ("sbuf", [128, 3 * CH], "float32"),
    "lw": ("sbuf", [128, 3 * SH], "float32"),
    "k1": ("sbuf", [128, CH], "float32"),
    "k2": ("sbuf", [128, CH], "float32"),
    "k3": ("sbuf", [128, CH], "float32"),
    "c1": ("sbuf", [128, CH], "float32"),
    "c2": ("sbuf", [128, CH], "float32"),
    "c3": ("sbuf", [128, CH], "float32"),
    "lu": ("sbuf", [128, 3 * SH], "uint16"),
    "lsend": ("dram", [128, 3], "uint16"),
    "lland": ("dram", [N * 128, 3], "uint16"),
    "comb": ("dram", [16, 3, 8 * N], "uint16"),
    "offs": ("sbuf", [128, 3 * 8 * N], "uint16"),
    "pw1": ("sbuf", [128, NP * WIN], "float32"),
    "pw2": ("sbuf", [128, NP * WIN], "float32"),
    "pw3": ("sbuf", [128, NP * WIN], "float32"),
    "y0": ("sbuf", [128, N * SH], "float32"),
    "y1": ("sbuf", [128, N * SH], "float32"),
    "y2": ("sbuf", [128, N * SH], "float32"),
    "y3": ("sbuf", [128, N * SH], "float32"),
    "pb": ("psum", [128, 512 * 8], "float32"),
}
SEMAPHORES = (["vs", "ss", "ps", "gs", "lix", "lwm", "ldl", "lx", "lbo", "st1", "st2", "sty", "stz", "loc", "lst",
               "hwc", "hwp", "hdc", "hdp"]
              + ["w%d" % q for q in range(N)] + ["d%d" % q for q in range(N)])


def bits(engines):
    m = 0
    for e in engines:
        m |= 1 << e
    return m


def links(src, dst, topo):
    a, b, d = topo.chip(src), topo.chip(dst), topo.die(src)
    out = []
    if not topo.same_plane(a, b):
        m = [c for c in range(topo.CHIPS) if topo.mates(a, c)][0]
        out.append(("mate", d, a))
        a = m
    if a != b:
        out.append(("out", d, a))
        out.append(("in", d, b))
    return out


def helpers(core, dsts, topo):
    ok = [c for c in topo.cores_of(core) if c != core and all(topo.may_write(c, d) for d in dsts)]
    near = [c for c in ok if topo.die(c) == topo.die(core)]
    far = [c for c in ok if topo.die(c) != topo.die(core)]
    return near[0], far[0]


def routes(cores, topo):
    hp = [helpers(c, [d for d in cores if d != c], topo) for c in cores]
    far = [[(q + 2) % N, (q + 4) % N] for q in range(N)]

    def cost(sel):
        load = {}
        for q in range(N):
            for r in range(N):
                if r != q:
                    s = hp[q][1] if r in sel[q] else cores[q]
                    for k in links(s, cores[r], topo):
                        load[k] = load.get(k, 0) + 1
        return (max(load.values()), sum(v * v for v in load.values()))

    best = cost(far)
    moved = True
    while moved:
        moved = False
        for q in range(N):
            for a in range(N):
                for b in range(a + 1, N):
                    if q in (a, b):
                        continue
                    for q2 in range(N):
                        for a2 in range(N):
                            for b2 in range(a2 + 1, N):
                                if q2 in (a2, b2) or (q2 == q and (a2, b2) != (a, b)) or q2 < q:
                                    continue
                                t = [list(f) for f in far]
                                t[q], t[q2] = [a, b], [a2, b2]
                                c = cost(t)
                                if c < best:
                                    best, far, moved = c, t, True
    near = [[r for r in range(N) if r != q and r not in far[q]] for q in range(N)]
    pick = None
    for n in range(3 ** N):
        ch = [near[q][n // 3 ** q % 3] for q in range(N)]
        if pick is None or len(set(ch)) > len(set(pick)):
            pick = ch
    return [(hp[q][0], hp[q][1], pick[q], [r for r in near[q] if r != pick[q]], far[q]) for q in range(N)]


_CACHE = {}


def plan(T, topo):
    if "r" not in _CACHE:
        _CACHE["r"] = routes(list(T.cores), topo)
    return _CACHE["r"]


def dst_id(c, topo):
    rid, pid, _ = topo.addr(c)
    return DstId(rid=rid, pnc=pid)


def u8(v):
    return v.bitcast(dt.uint8)


def helper_program(g, core, T, topo, q, ranks):
    dst = [T.cores[r] for r in ranks]
    ids = [dst_id(c, topo) for c in dst]
    eng = [e for e in topo.engines(core, dst[0]) if all(e in topo.engines(core, d) for d in dst)]
    wc, dc = slice(SH * q, SH * (q + 1)), slice(3 * CH * q, 3 * CH * (q + 1))
    n = 0
    for arr, src, out, sem in ((T.sem.hwc, u8(T.hw[:]), u8(T.wl[:, wc]), "w%d" % q),
                               (T.sem.hwp, T.hws[:], T.ws[:, wc], "w%d" % q),
                               (T.sem.hdc, u8(T.hd[:]), u8(T.dq[:, dc]), "d%d" % q),
                               (T.sem.hdp, T.hds[:], T.dp[:, dc], "d%d" % q)):
        g.wait_ge(arr, 8)
        g.remote_dma_fused([RemoteDMATransfer(dst_ids=ids, dma_engine_mask=bits(eng), remote_sem=T.sem[sem],
                                              srcs=[src], dsts=[out for _ in dst])], local_sem=T.sem.loc)
        n += len(eng)
    g.wait_ge(T.sem.loc, n)


def rank_program(g, core, T, topo):
    P = plan(T, topo)
    r = T.rank_of(core)
    if r is None:
        for q in range(N):
            if core == P[q][0]:
                helper_program(g, core, T, topo, q, P[q][3])
            if core == P[q][1]:
                helper_program(g, core, T, topo, q, P[q][4])
        return
    near, far, direct, _, _ = P[r]
    odd = r % 2
    mcol = 0 if odd else 512
    dcol = [None] + [(320 + CH * (k - 1)) if odd else (320 - CH * k) for k in (1, 2, 3)]
    dlow = 320 if odd else 128
    gap = (128, 320) if odd else (320, 512)
    org = [None, mcol, 0 if odd else dcol[1], 0 if odd else dcol[2]]
    end = [None, mcol + SH, dcol[1] + CH if odd else WIN, dcol[2] + CH if odd else WIN]
    add, mult = AluOpType.add, AluOpType.mult
    cnt = {"v": 0, "s": 0, "p": 0, "g": 0}
    sem = {"v": T.sem.vs, "s": T.sem.ss, "p": T.sem.ps, "g": T.sem.gs}
    queue = {"v": g.vector, "s": g.scalar, "p": g.tensor, "g": g, "y": g.sync}
    seen = {}

    def done(k, ins):
        ins.then_inc(sem[k], 1)
        cnt[k] += 1
        return cnt[k]

    def wait(on, s, val):
        key = (on, s)
        if seen.get(key, 0) < val:
            seen[key] = val
            queue[on].wait_ge(sem[s] if s in sem else T.sem[s], val)

    v, sc, y, te = g.vector, g.scalar, g.sync, g.tensor
    wc, dc = slice(SH * r, SH * (r + 1)), slice(3 * CH * r, 3 * CH * (r + 1))

    for k in range(4):
        y.dma_start(T.ix[16 * k:16 * k + 16, :], T.idx[:]).then_inc(T.sem.lix, 16)
        sc.dma_start(T.ix[64 + 16 * k:64 + 16 * k + 16, :], T.idx[:]).then_inc(T.sem.lix, 16)
    y.dma_start(T.md[:, 4 * mcol:4 * mcol + 512], T.wm[:]).then_inc(T.sem.lwm, 16)
    sc.dma_start(T.dlt[:], T.dl[:]).then_inc(T.sem.ldl, 16)
    y.dma_start(T.xt[:], T.x[:]).then_inc(T.sem.lx, 16)

    g_pi = done("g", g.iota(T.pi[:], [[0, 1]], 0, 1))
    g_mi = done("g", g.iota(T.mi[:], [[-4, CH]], 4 * CH, 1))
    g_lw = done("g", g.iota(T.lw[:], [[1, 16], [0, 3], [16, 8]], mcol, 0, allow_small_or_imprecise_dtypes=True))
    g_vl = done("g", g.iota(T.vl[:], [[CH if odd else -CH, 3], [1, CH]], dcol[1], 0, allow_small_or_imprecise_dtypes=True))
    g_rm = done("g", g.iota(T.rm[:], [[0, 16], [1024, 4]], 0, 0, allow_small_or_imprecise_dtypes=True))

    done("v", v.memset(T.md[:, 4 * gap[0]:4 * gap[1]], 0.0))
    wait("v", "g", g_mi)
    v_pe = done("v", v.tensor_scalar(T.pe[:], T.pi[:], 3, None, AluOpType.bitwise_and))
    v_mj = done("v", v.tensor_scalar(T.mj[:], T.mi[:], 2, 3, AluOpType.arith_shift_right, AluOpType.bitwise_and))
    wait("v", "v", v_pe)
    for k in (1, 2, 3):
        done("v", v.tensor_scalar(T["e%d" % k][:], T.pe[:], -4 * org[k], None, add))
    wait("v", "v", v_mj)
    done("v", v.tensor_scalar(T.mk[:], T.mj[:], 0, None, AluOpType.is_equal))
    wait("v", "lix", 128)
    v_lo = done("v", v.tensor_scalar(T.lo[:], T.ix[:], 15, None, AluOpType.bitwise_and))
    done("v", v.tensor_scalar(T.hi[:], T.ix[:], 4, None, AluOpType.arith_shift_right))
    wait("v", "v", v_lo)
    a = done("v", v.tensor_scalar(T.lm[:], T.lo[:], 24, None, mult))
    wait("v", "v", a)
    a = done("v", v.tensor_tensor(T.sm[:], T.lm[:], T.hi[:], add))
    wait("v", "v", a)
    done("v", v.tensor_copy(T.piu[:], T.sm[:]))

    def place(k, t):
        wait("v", "v", cnt["v"])
        return done("v", v.tensor_copy(T.lw[:, 8 * (t - 1):3 * SH].indirect(T.piu[:, 4 * (k - 1):4 * k]),
                                       T.vl[:, CH * (k - 1):CH * k]))

    def look(t, k):
        wait("v", "v", cnt["v"])
        return done("v", v.tensor_tensor(T["k%d" % k][:], T.lw[:, 8 * (t - 1):3 * SH].indirect(T.piu[:, 4 * (k - 1):4 * k]),
                                         T.mk[:], mult))

    wait("v", "g", g_rm)
    look(3, 1)
    place(1, 1)
    look(1, 2)
    wait("v", "lwm", 16)
    v_qw = done("v", v.quantize_mx(T.wl[:, wc], T.ws[:, wc], T.md[:, 4 * mcol:4 * mcol + 512]))
    place(1, 2)
    place(2, 2)
    look(2, 3)
    place(1, 3)
    place(2, 3)
    place(3, 3)
    wait("v", "v", cnt["v"])
    v_lu = done("v", v.tensor_copy(T.lu[0:1, :], T.lw[0:1, :]))
    scan = {}
    for k in (1, 2, 3):
        scan[k] = done("v", v.tensor_tensor_scan(T["c%d" % k][:], T.rm[:], T["k%d" % k][:], 0.0, AluOpType.min, add))
    for k in (1, 2, 3):
        wait("v", "v", scan[k])
        done("v", v.tensor_scalar(T["o%d" % k][:], T["c%d" % k][:, 3:CH:4], 4, T["e%d" % k][:], mult, add))
    for k in (1, 2, 3):
        wait("v", "v", cnt["v"])
        wait("v", "s", k)
        done("v", v.tensor_tensor(T.md[:, 4 * dcol[k]:4 * dcol[k] + 4 * CH],
                                  T.md[:, 4 * org[k]:4 * end[k]].indirect(T["o%d" % k][:]),
                                  T.dls[:, 4 * CH * (k - 1):4 * CH * k], add))
    wait("v", "v", cnt["v"])
    v_qd = done("v", v.quantize_mx(T.dq[:, dc], T.dp[:, dc], T.md[:, 4 * dlow:4 * dlow + 12 * CH]))
    wait("v", "lx", 16)
    v_qx = done("v", v.quantize_mx(T.xq[:], T.xs[:], T.xt[:]))
    for p in range(NP):
        for t in (1, 2):
            for lo, hi in ((128, 320 - CH * t), (320 + CH * t, 512)):
                v_ms = done("v", v.memset(T["pw%d" % t][:, WIN * p + lo:WIN * p + hi], 0.0))

    wait("s", "ldl", 16)
    for k in range(3):
        sl = slice(4 * CH * k, 4 * CH * (k + 1))
        done("s", sc.activation(T.dls[:, sl], T.dlt[:, sl], ActivationFunctionType.Copy, scale=0.25))

    onchip = topo.engines(core, far)
    ef, en = onchip[0::2], onchip[1::2]
    drk = T.cores[direct]
    ed = topo.engines(core, drk)
    nloc = [0]

    def hand(src, out, s):
        g.remote_dma_fused([RemoteDMATransfer(dst_ids=[dst_id(far, topo)], dma_engine_mask=bits(ef), remote_sem=T.sem[s],
                                              srcs=[src], dsts=[out]),
                            RemoteDMATransfer(dst_ids=[dst_id(near, topo)], dma_engine_mask=bits(en), remote_sem=T.sem[s],
                                              srcs=[src], dsts=[out])], local_sem=T.sem.loc)
        nloc[0] += len(ef) + len(en)

    def send(view, s):
        g.remote_dma_fused([RemoteDMATransfer(dst_ids=[dst_id(drk, topo)], dma_engine_mask=bits(ed), remote_sem=T.sem[s],
                                              srcs=[view], dsts=[view])], local_sem=T.sem.loc)
        nloc[0] += len(ed)

    wait("g", "v", v_qw)
    hand(u8(T.wl[:, wc]), u8(T.hw[:]), "hwc")
    hand(T.ws[:, wc], T.hws[:], "hwp")
    send(u8(T.wl[:, wc]), "w%d" % r)
    send(T.ws[:, wc], "w%d" % r)
    others = [T.cores[q] for q in range(N) if q != r]
    land = T.lland[128 * r:128 * (r + 1), :]
    wait("g", "lbo", 16)
    g.remote_dma_fused([RemoteDMATransfer(dst_ids=[dst_id(c, topo) for c in others], dma_engine_mask=bits(ed[:1]),
                                          remote_sem=T.sem.lst, srcs=[T.lsend[:]], dsts=[land for _ in others])],
                       local_sem=T.sem.loc)
    nloc[0] += 1
    wait("g", "v", v_qd)
    hand(u8(T.dq[:, dc]), u8(T.hd[:]), "hdc")
    hand(T.dp[:, dc], T.hds[:], "hdp")
    send(u8(T.dq[:, dc]), "d%d" % r)
    send(T.dp[:, dc], "d%d" % r)

    wait("y", "v", v_lu)
    y.dma_start(T.lsend[:], T.lu[0:1, :]).then_inc(T.sem.lbo, 16)
    wait("y", "lbo", 16)
    y.dma_start(T.comb[:, :, 8 * r:8 * r + 8], T.lsend[:]).then_inc(T.sem.st1, 16)
    wait("y", "lst", N - 1)
    for q in range(N):
        if q != r:
            y.dma_start(T.comb[:, :, 8 * q:8 * q + 8], T.lland[128 * q:128 * (q + 1), :]).then_inc(T.sem.st1, 16)
    wait("y", "st1", 16 * N)
    for k in range(8):
        y.dma_start(T.offs[16 * k:16 * k + 16, :], T.comb[:]).then_inc(T.sem.st2, 16)

    order = [(r // 2 + k) % NP for k in range(NP)]
    units = [("w", p, t) for p in order for t in range(RD)] + [("d", p, t) for p in order for t in (1, 3, 2)]
    eng = {u: (("s" if u[2] in (0, 2) else "v") if u[0] == "w" else ("v" if u[2] == 3 else "s")) for u in units}
    bank, use = {}, {"v": 0, "s": 0}
    for u in units:
        e = eng[u]
        bank[u] = (0 if e == "v" else 4) + use[e] % 4
        use[e] += 1
    num = {u: i + 1 for i, u in enumerate(units)}

    def ps(u, lo, hi):
        return T.pb[:, 512 * bank[u] + lo:512 * bank[u] + hi]

    def copy(e, out, in_):
        return done(e, v.tensor_copy(out, in_) if e == "v" else sc.activation(out, in_, ActivationFunctionType.Copy))

    drained, got, shard = {}, {}, {}

    def drain(e, u):
        kind, p, t = u
        wait(e, "p", num[u])
        if kind == "w" and t == 0:
            drained[u] = copy(e, T.y0[:, 256 * p:256 * p + 256], ps(u, 0, 256))
        elif kind == "w":
            copy(e, T["pw%d" % t][:, WIN * p + 512:WIN * p + 640], ps(u, 0, 128))
            drained[u] = copy(e, T["pw%d" % t][:, WIN * p:WIN * p + 128], ps(u, 128, 256))
            shard[(p, t)] = (e, drained[u])
        else:
            drained[u] = copy(e, T["pw%d" % t][:, WIN * p + 320 - CH * t:WIN * p + 320 + CH * t], ps(u, 0, 128 * t))

    def gather(e, p, t):
        wait(e, "st2", 128)
        wait(e, "v", v_ms)
        wait(e, shard[(p, t)][0], shard[(p, t)][1])
        wait(e, eng[("d", p, t)], drained[("d", p, t)])
        win = T["pw%d" % t][:, WIN * p:WIN * p + WIN].indirect(T.offs[:, 48 * (t - 1) + 16 * p:48 * (t - 1) + 16 * p + 16])
        got[(p, t)] = (e, copy(e, T["y%d" % t][:, 256 * p:256 * p + 256], win))

    for p in order:
        drain("s", ("w", p, 0))
        drain("s", ("w", p, 2))
        wait("s", "s", drained[("w", p, 0)])
        sc.dma_start(T.y[:, 256 * p:256 * p + 256], T.y0[:, 256 * p:256 * p + 256]).then_inc(T.sem.sty, 16)
        drain("v", ("w", p, 1))
        drain("v", ("w", p, 3))
    A, B, C = order
    for p in (A, B):
        drain("s", ("d", p, 1))
        drain("s", ("d", p, 2))
        drain("v", ("d", p, 3))
    gather("v", A, 1)
    gather("v", A, 3)
    gather("s", A, 2)
    gather("v", B, 3)
    gather("s", B, 1)
    gather("s", B, 2)
    drain("s", ("d", C, 1))
    drain("s", ("d", C, 2))
    drain("v", ("d", C, 3))
    gather("s", C, 2)
    gather("v", C, 1)
    gather("v", C, 3)

    wait("p", "v", v_qx)
    last = {}
    for u in units:
        kind, p, t = u
        for q in (2 * p, 2 * p + 1):
            if q != r:
                wait("p", ("w%d" if kind == "w" else "d%d") % q, 16)
        b = bank[u]
        if b in last:
            wait("p", eng[u], drained[last[b]])
        last[b] = u
        if kind == "w":
            n, lo = 256, 256 * p
            codes, scales = T.wl, T.ws
        else:
            n, lo = 128 * t, 384 * p + 192 - CH * t
            codes, scales = T.dq, T.dp
        done("p", te.matmul_mx(ps(u, 0, n), T.xq[:, 128 * t:128 * t + 128], T.xs[:, 128 * t:128 * t + 128],
                               codes[:, lo:lo + n], scales[:, lo:lo + n], True, True))

    for p, t in ((A, 1), (A, 2), (A, 3), (B, 1), (B, 3), (B, 2), (C, 1), (C, 2), (C, 3)):
        e, k = got[(p, t)]
        wait("y", e, k)
        y.dma_start(T.y[:, SH * N * t + 256 * p:SH * N * t + 256 * p + 256],
                    T["y%d" % t][:, 256 * p:256 * p + 256]).then_inc(T.sem.stz, 16)

    wait("g", "loc", nloc[0])
    for k in ("g", "v", "s", "p"):
        wait("g", k, cnt[k])
    wait("g", "st2", 128)
    wait("g", "sty", 16 * NP)
    wait("g", "stz", 16 * 3 * NP)
